import numpy as np
import ml_dtypes


def mxq(x, axis, fmt="e4m3"):
    dtype, down = {"e4m3": (ml_dtypes.float8_e4m3fn, 7), "e5m2": (ml_dtypes.float8_e5m2, 14)}[fmt]
    v = np.moveaxis(np.asarray(x, np.float32).astype(ml_dtypes.bfloat16).astype(np.float64), axis, -1)
    blocks = v.reshape(v.shape[:-1] + (-1, 32))
    amax = np.abs(blocks).max(-1, keepdims=True)
    byte = np.maximum(np.where(amax > 0, np.frexp(amax)[1] - 1 + 127, 0) - down, 1)
    scale = np.exp2(byte - 127.0)
    codes = (blocks / scale).astype(np.float32).astype(dtype).astype(np.float64)
    return np.moveaxis((codes * scale).reshape(v.shape), -1, axis)


WIDE = False


def mx_kscale(k):
    if not WIDE:
        return np.ones(k)
    levels = np.array([10, -10, 5, -5, 0])
    if k % 512:
        return np.exp2(np.random.permutation(np.resize(levels, k // 32))).repeat(32)
    a = np.empty((k // 512, 16))
    for p in range(k // 512):
        a[p, :8] = np.random.permutation(np.resize(levels, 8))
        for g in range(8):
            far = levels[np.abs(levels - a[p, g]) >= 10]
            a[p, g + 8] = far[np.random.randint(len(far))]
    return np.exp2(a.ravel()).repeat(32)


def f64(x):
    return np.asarray(x).astype(np.float64)


def striped(idx):
    return np.tile(idx.reshape(-1, 16).T, (8, 1)).astype(np.uint16)


def unstriped(offs):
    return offs[:16].T.reshape(-1).astype(np.int64)


E2M1 = np.array([0.0, 0.5, 1.0, 1.5, 2.0, 3.0, 4.0, 6.0, -0.0, -0.5, -1.0, -1.5, -2.0, -3.0, -4.0, -6.0])


def pack_weight(w, fmt):
    k, n = w.shape
    w = f64(np.asarray(w, np.float32).astype(ml_dtypes.bfloat16)).reshape(k // 32, 32, n)
    amax = np.abs(w).max(1)
    if fmt == "e4m3":
        byte = np.frexp(amax)[1] - 1 + 127 - 7
    else:
        mant, ex = np.frexp(amax / 6.0)
        byte = np.where(mant > 0.5, ex, ex - 1) + 127
    byte = np.clip(np.where(amax > 0, byte, 1), 1, 254)
    scaled = (w * np.exp2(127.0 - byte)[:, None, :]).reshape(k, n).astype(np.float32)
    by_word = np.ascontiguousarray(scaled.reshape(k // 512, 128, 4, n).transpose(0, 1, 3, 2))
    if fmt == "e4m3":
        words = by_word.astype(ml_dtypes.float8_e4m3fn).view(np.uint8)
    else:
        c = by_word.astype(ml_dtypes.float4_e2m1fn).view(np.uint8) & 0xF
        words = (c[..., 0::2] | (c[..., 1::2] << 4)).reshape(k // 512, 128, 2 * n)
    return np.ascontiguousarray(words), np.ascontiguousarray(byte.astype(np.uint8).reshape(k // 512, 16, n))


def unpack_weight(words, scales, fmt):
    g, _, n = scales.shape
    words = np.ascontiguousarray(words).reshape(g, 128, n, -1)
    if fmt == "e4m3":
        vals = words.view(ml_dtypes.float8_e4m3fn).astype(np.float64)
    else:
        nib = np.empty((g, 128, n, 4), np.uint8)
        nib[..., 0::2] = words & 0xF
        nib[..., 1::2] = words >> 4
        vals = E2M1[nib]
    vals = vals * np.repeat(np.exp2(scales.astype(np.float64) - 127.0), 8, axis=1)[..., None]
    return vals.transpose(0, 1, 3, 2).reshape(g * 512, n)


def pack_table4(v):
    words, scales = pack_weight(v, "e2m1")
    g, t = words.shape[0] // 2, v.shape[1]
    words = words.reshape(g, 2, 128, t, 2).transpose(0, 2, 3, 1, 4)
    return np.concatenate([words.reshape(g, -1), scales.reshape(g, -1)], axis=1)


def unpack_table4(tab):
    g, t = tab.shape[0], tab.shape[1] // 544
    words = tab[:, :512 * t].reshape(g, 128, t, 2, 2).transpose(0, 3, 1, 2, 4).reshape(2 * g, 128, 2 * t)
    return unpack_weight(words, tab[:, 512 * t:].reshape(2 * g, 16, t), "e2m1")


def pack_table(v):
    words, scales = pack_weight(v, "e4m3")
    return np.concatenate([words.reshape(words.shape[0], -1), scales.reshape(scales.shape[0], -1)], axis=1)


def unpack_table(tab):
    g, t = tab.shape[0], tab.shape[1] // 528
    return unpack_weight(tab[:, :512 * t].reshape(g, 128, t, 4), tab[:, 512 * t:].reshape(g, 16, t), "e4m3")


K, L, M, T, S = 1536, 1024, 128, 1024, 512


def setup_inputs():
    n = np.random.standard_normal
    s1 = mx_kscale(K)[:, None]
    s2 = mx_kscale(L)[:, None]
    p_w4 = pack_weight(n((K, M)) / np.sqrt(K) / s1, "e2m1")
    return {
        "tab": pack_table(n((K, T)) * s1),
        "w4_words": p_w4[0],
        "w4_scales": p_w4[1],
        "tab2": pack_table4(n((L, T)) * s2),
        "u": (n((L, M)) / np.sqrt(L) / s2).astype(np.float32),
        "offs": striped(np.random.permutation(T)[:S]),
        "offs2": striped(np.random.permutation(T)[:S]),
    }


def reference(tab, w4_words, w4_scales, tab2, u, offs, offs2):
    tab_ = unpack_table(tab)[:, unstriped(offs)]
    w4_ = unpack_weight(w4_words, w4_scales, "e2m1")
    tab2_ = unpack_table4(tab2)[:, unstriped(offs2)]
    u_ = mxq(f64(u), 0, "e4m3")
    y = w4_.T @ tab_ + u_.T @ tab2_
    return y

@@ -1,0 +1,139 @@
+from contextlib import ExitStack
+
+import concourse.mybir as mybir
+
+F32 = mybir.dt.float32
+BF16 = mybir.dt.bfloat16
+I32 = mybir.dt.int32
+U32 = mybir.dt.uint32
+U16 = mybir.dt.uint16
+U8 = mybir.dt.uint8
+FP8X4 = mybir.dt.float8_e4m3fn_x4
+FP4X4 = mybir.dt.float4_e2m1fn_x4
+
+P = 128
+K, L, M, T, S = 1536, 1024, 128, 1024, 512
+KP = K // 512
+LP = L // 512
+QUAD = 32
+GROUP = 128
+GROUPS = S // GROUP
+FLOPS = 2 * M * S * (K + L)
+
+
+def tile_list_tab48_none_kernel(tc, tab, w4_words, w4_scales, tab2, u, offs, offs2, out):
+    nc = tc.nc
+    with ExitStack() as ctx:
+        keep = ctx.enter_context(tc.tile_pool(name="keep", bufs=1))
+        psum = ctx.enter_context(tc.psum_pool(name="psum", bufs=1))
+
+        list1 = keep.tile([P, S // 16], U16, name="list1")
+        list2 = keep.tile([P, S // 16], U16, name="list2")
+        sc2 = keep.tile([P, T // 4], I32, name="sc2", align_bytes=64)
+        sc1 = keep.tile([P, KP, T // 4], I32, name="sc1", align_bytes=64)
+        words2 = keep.tile([P, T], I32, name="words2", align_bytes=64)
+        words1 = [keep.tile([P, T], I32, name=f"words1_{a}", align_bytes=64) for a in range(KP)]
+        u_raw = keep.tile([P, LP, 4, M], F32, name="u_raw", align_bytes=64)
+        u_bf = keep.tile([P, LP, M, 4], BF16, name="u_bf", align_bytes=64)
+        u_codes = keep.tile([P, LP * M], U32, name="u_codes", align_bytes=64)
+        u_scales = keep.tile([P, LP * M], U8, name="u_scales", align_bytes=64)
+        w_words = keep.tile([P, KP, 2 * M], U8, name="w_words", align_bytes=64)
+        w_sc = keep.tile([P, KP, M // 4], I32, name="w_sc", align_bytes=64)
+        g_words2 = keep.tile([P, S], U32, name="g_words2", align_bytes=64)
+        parted2 = keep.tile([P, LP * 2 * S], U8, name="parted2", align_bytes=64)
+        g_sc2 = keep.tile([P, S], U8, name="g_sc2", align_bytes=64)
+        shifted2 = keep.tile([P, S // 4], I32, name="shifted2", align_bytes=64)
+        g_words1 = [keep.tile([P, S], U32, name=f"g_words1_{a}", align_bytes=64) for a in range(KP)]
+        g_sc1 = [keep.tile([P, S], U8, name=f"g_sc1_{a}", align_bytes=64) for a in range(KP)]
+        out_a = keep.tile([P, S - GROUP], F32, name="out_a", align_bytes=64)
+        out_b = keep.tile([P, GROUP], F32, name="out_b", align_bytes=64)
+        banks = [psum.tile([P, 512], F32, name=f"bank{g}") for g in range(GROUPS)]
+
+        nc.gpsimd.memset(sc2[:], 0)
+        nc.vector.memset(sc1[:], 0)
+        nc.gpsimd.memset(shifted2[:], 0)
+        nc.gpsimd.memset(w_sc[:], 0)
+
+        def load_words(eng, tile, src):
+            eng.dma_start(tile[:], src[0 : 512 * T].rearrange("(p b) -> p b", p=P).bitcast(I32))
+
+        tab2_sc = tab2[0, 512 * T :].rearrange("(h q t) -> h q t", h=LP, q=16)
+        tab_sc = tab[:, 512 * T :].rearrange("a (q t) -> q a t", q=16)
+        w_sc_src = w4_scales.rearrange("a q n -> q a n")
+        nc.sync.dma_start(list2[:], offs2)
+        nc.sync.dma_start(sc2[4:20, :], tab2_sc[1].bitcast(I32))
+        for q in range(4):
+            nc.sync.dma_start(sc2[QUAD * q : QUAD * q + 4, :], tab2_sc[0, 4 * q : 4 * q + 4, :].bitcast(I32))
+        load_words(nc.sync, words2, tab2[0])
+        nc.sync.dma_start(list1[:], offs)
+        nc.sync.dma_start(u_raw[:].rearrange("p h j n -> p h (j n)"), u.rearrange("(h p j) n -> p h (j n)", h=LP, j=4))
+        for q in range(4):
+            nc.sync.dma_start(sc1[QUAD * q : QUAD * q + 4, :, :], tab_sc[4 * q : 4 * q + 4].bitcast(I32))
+        for a in range(KP):
+            load_words(nc.sync, words1[a], tab[a])
+        nc.gpsimd.dma_start(w_words[:].bitcast(I32), w4_words.rearrange("a p b -> p a b").bitcast(I32))
+        for q in range(4):
+            nc.gpsimd.dma_start(w_sc[QUAD * q : QUAD * q + 4, :, :], w_sc_src[4 * q : 4 * q + 4].bitcast(I32))
+
+        nc.scalar.copy(u_bf[:], u_raw[:].rearrange("p h j n -> p h n j"))
+
+        nc.vector.tensor_copy(g_sc2[:], sc2[:].bitcast(U8).indirect(list2[:]))
+        for q in range(4):
+            nc.scalar.dma_start(shifted2[QUAD * q : QUAD * q + 4, :], g_sc2[4 + 4 * q : 8 + 4 * q, :].bitcast(I32))
+        nc.vector.tensor_copy(g_words2[:], words2[:].bitcast(U32).indirect(list2[:]))
+        nc.vector.tensor_copy(
+            parted2[:].bitcast(U16).rearrange("p (h n) -> p h n", h=LP),
+            g_words2[:].bitcast(U16).rearrange("p (n h) -> p h n", h=LP),
+        )
+        sc1_u8 = sc1[:].rearrange("p a t -> p (a t)").bitcast(U8)
+        nc.vector.tensor_copy(g_sc1[0][:], sc1_u8[:, 0:T].indirect(list1[:]))
+        nc.vector.quantize_mx(
+            out=u_codes[:].bitcast(FP8X4),
+            scales=u_scales[:],
+            in_=u_bf[:].rearrange("p h n j -> p (h n j)"),
+        )
+        shifted2_u8 = shifted2[:].bitcast(U8)
+        for h in range(LP):
+            plane = (g_sc2[:], shifted2_u8)[h]
+            for g in range(GROUPS):
+                nc.tensor.matmul_mx(
+                    out=banks[g][:, 0:GROUP],
+                    lhsT=u_codes[:, M * h : M * (h + 1)].bitcast(FP8X4),
+                    lhsT_scale=u_scales[:, M * h : M * (h + 1)],
+                    rhs=parted2[:, 2 * S * h + 2 * GROUP * g : 2 * S * h + 2 * GROUP * (g + 1)].bitcast(FP4X4),
+                    rhs_scale=plane[:, GROUP * g : GROUP * (g + 1)],
+                    start=(h == 0),
+                    stop=False,
+                )
+        for a in range(1, KP):
+            nc.vector.tensor_copy(g_sc1[a][:], sc1_u8[:, T * a : T * (a + 1)].indirect(list1[:]))
+
+        w_sc_u8 = w_sc[:].rearrange("p a n -> p (a n)").bitcast(U8)
+
+        def multiply(a, g):
+            nc.tensor.matmul_mx(
+                out=banks[g][:, 0:GROUP],
+                lhsT=w_words[:, a, :].bitcast(FP4X4),
+                lhsT_scale=w_sc_u8[:, M * a : M * (a + 1)],
+                rhs=g_words1[a][:, GROUP * g : GROUP * (g + 1)].bitcast(FP8X4),
+                rhs_scale=g_sc1[a][:, GROUP * g : GROUP * (g + 1)],
+                start=False,
+                stop=(a == KP - 1),
+            )
+
+        for a in range(KP - 1):
+            nc.vector.tensor_copy(g_words1[a][:], words1[a][:].bitcast(U32).indirect(list1[:]))
+            for g in range(GROUPS):
+                multiply(a, g)
+        a = KP - 1
+        cut = S - GROUP
+        nc.vector.tensor_copy(g_words1[a][:, 0:cut], words1[a][:].bitcast(U32).indirect(list1[:, 0 : cut // 16]))
+        for g in range(GROUPS - 1):
+            multiply(a, g)
+        nc.vector.tensor_copy(g_words1[a][:, cut:S], words1[a][:].bitcast(U32).indirect(list1[:, cut // 16 :]))
+        multiply(a, GROUPS - 1)
+        for g in range(GROUPS - 1):
+            nc.scalar.copy(out_a[:, GROUP * g : GROUP * (g + 1)], banks[g][:, 0:GROUP])
+        nc.sync.dma_start(out[:, 0:cut], out_a[:])
+        nc.vector.tensor_copy(out_b[:], banks[GROUPS - 1][:, 0:GROUP])
+        nc.sync.dma_start(out[:, cut:S], out_b[:])

@@ -30,12 +30,11 @@ def tile_list_tab48_none_kernel(tc, tab, w4_words, w4_scales, tab2, u, offs, off
         list1 = keep.tile([P, S // 16], U16, name="list1")
         list2 = keep.tile([P, S // 16], U16, name="list2")
         sc2 = keep.tile([P, T // 4], I32, name="sc2", align_bytes=64)
-        sc1 = keep.tile([P, KP, T // 4], I32, name="sc1", align_bytes=64)
+        sc1 = keep.tile([P, KP, T // 4], I32, name="sc1", tag="turns", align_bytes=64)
         words2 = keep.tile([P, T], I32, name="words2", align_bytes=64)
         words1 = [keep.tile([P, T], I32, name=f"words1_{a}", align_bytes=64) for a in range(KP)]
         u_raw = keep.tile([P, LP, 4, M], F32, name="u_raw", align_bytes=64)
         u_bf = keep.tile([P, LP, M, 4], BF16, name="u_bf", align_bytes=64)
-        u_codes = keep.tile([P, LP * M], U32, name="u_codes", align_bytes=64)
         u_scales = keep.tile([P, LP * M], U8, name="u_scales", align_bytes=64)
         w_words = keep.tile([P, KP, 2 * M], U8, name="w_words", align_bytes=64)
         w_sc = keep.tile([P, KP, M // 4], I32, name="w_sc", align_bytes=64)
@@ -66,7 +65,7 @@ def tile_list_tab48_none_kernel(tc, tab, w4_words, w4_scales, tab2, u, offs, off
             nc.sync.dma_start(sc2[QUAD * q : QUAD * q + 4, :], tab2_sc[0, 4 * q : 4 * q + 4, :].bitcast(I32))
         load_words(nc.sync, words2, tab2[0])
         nc.sync.dma_start(list1[:], offs)
-        nc.sync.dma_start(u_raw[:].rearrange("p h j n -> p h (j n)"), u.rearrange("(h p j) n -> p h (j n)", h=LP, j=4))
+        nc.gpsimd.dma_start(u_raw[:].rearrange("p h j n -> p h (j n)"), u.rearrange("(h p j) n -> p h (j n)", h=LP, j=4))
         for q in range(4):
             nc.sync.dma_start(sc1[QUAD * q : QUAD * q + 4, :, :], tab_sc[4 * q : 4 * q + 4].bitcast(I32))
         for a in range(KP):
@@ -81,12 +80,14 @@ def tile_list_tab48_none_kernel(tc, tab, w4_words, w4_scales, tab2, u, offs, off
         for q in range(4):
             nc.scalar.dma_start(shifted2[QUAD * q : QUAD * q + 4, :], g_sc2[4 + 4 * q : 8 + 4 * q, :].bitcast(I32))
         nc.vector.tensor_copy(g_words2[:], words2[:].bitcast(U32).indirect(list2[:]))
+        sc1_u8 = sc1[:].rearrange("p a t -> p (a t)").bitcast(U8)
+        for a in range(KP):
+            nc.vector.tensor_copy(g_sc1[a][:], sc1_u8[:, T * a : T * (a + 1)].indirect(list1[:]))
         nc.vector.tensor_copy(
             parted2[:].bitcast(U16).rearrange("p (h n) -> p h n", h=LP),
             g_words2[:].bitcast(U16).rearrange("p (n h) -> p h n", h=LP),
         )
-        sc1_u8 = sc1[:].rearrange("p a t -> p (a t)").bitcast(U8)
-        nc.vector.tensor_copy(g_sc1[0][:], sc1_u8[:, 0:T].indirect(list1[:]))
+        u_codes = keep.tile([P, LP * M], U32, name="u_codes", tag="turns", align_bytes=64)
         nc.vector.quantize_mx(
             out=u_codes[:].bitcast(FP8X4),
             scales=u_scales[:],
@@ -105,8 +106,6 @@ def tile_list_tab48_none_kernel(tc, tab, w4_words, w4_scales, tab2, u, offs, off
                     start=(h == 0),
                     stop=False,
                 )
-        for a in range(1, KP):
-            nc.vector.tensor_copy(g_sc1[a][:], sc1_u8[:, T * a : T * (a + 1)].indirect(list1[:]))
 
         w_sc_u8 = w_sc[:].rearrange("p a n -> p (a n)").bitcast(U8)
 

@@ -48,45 +48,47 @@ def tile_list_tab48_none_kernel(tc, tab, w4_words, w4_scales, tab2, u, offs, off
         out_b = keep.tile([P, GROUP], F32, name="out_b", align_bytes=64)
         banks = [psum.tile([P, 512], F32, name=f"bank{g}") for g in range(GROUPS)]
 
-        nc.gpsimd.memset(sc2[:], 0)
-        nc.vector.memset(sc1[:], 0)
         nc.gpsimd.memset(shifted2[:], 0)
-        nc.gpsimd.memset(w_sc[:], 0)
+        nc.vector.memset(sc1[:], 0)
+        for a in range(KP):
+            nc.vector.memset(words1[a][:, 0:1], 0)
+        nc.vector.memset(w_sc[:], 0)
 
         def load_words(eng, tile, src):
             eng.dma_start(tile[:], src[0 : 512 * T].rearrange("(p b) -> p b", p=P).bitcast(I32))
 
-        tab2_sc = tab2[0, 512 * T :].rearrange("(h q t) -> h q t", h=LP, q=16)
-        tab_sc = tab[:, 512 * T :].rearrange("a (q t) -> q a t", q=16)
-        w_sc_src = w4_scales.rearrange("a q n -> q a n")
         nc.sync.dma_start(list2[:], offs2)
-        nc.sync.dma_start(sc2[4:20, :], tab2_sc[1].bitcast(I32))
-        for q in range(4):
-            nc.sync.dma_start(sc2[QUAD * q : QUAD * q + 4, :], tab2_sc[0, 4 * q : 4 * q + 4, :].bitcast(I32))
+        tab2_sc = tab2[0, 512 * T :].rearrange("(r t) -> r t", t=T).bitcast(I32)
+        nc.sync.dma_start(sc2[0:QUAD, :], tab2_sc)
+        for q in range(1, 4):
+            rows = tab2_sc[4 * q : 4 * q + 4, :].unsqueeze(0).to_broadcast([8, 4, T // 4])
+            nc.sync.dma_start(sc2[QUAD * q : QUAD * (q + 1), :], rows)
         load_words(nc.sync, words2, tab2[0])
         nc.sync.dma_start(list1[:], offs)
         nc.gpsimd.dma_start(u_raw[:].rearrange("p h j n -> p h (j n)"), u.rearrange("(h p j) n -> p h (j n)", h=LP, j=4))
+        nc.gpsimd.dma_start(w_words[:].bitcast(I32), w4_words.rearrange("a p b -> p a b").bitcast(I32))
+        tab_sc = tab[:, 512 * T :].rearrange("a (q t) -> q a t", q=16)
         for q in range(4):
             nc.sync.dma_start(sc1[QUAD * q : QUAD * q + 4, :, :], tab_sc[4 * q : 4 * q + 4].bitcast(I32))
         for a in range(KP):
             load_words(nc.sync, words1[a], tab[a])
-        nc.gpsimd.dma_start(w_words[:].bitcast(I32), w4_words.rearrange("a p b -> p a b").bitcast(I32))
+        w_sc_src = w4_scales.rearrange("a q n -> q a n")
         for q in range(4):
-            nc.gpsimd.dma_start(w_sc[QUAD * q : QUAD * q + 4, :, :], w_sc_src[4 * q : 4 * q + 4].bitcast(I32))
+            nc.sync.dma_start(w_sc[QUAD * q : QUAD * q + 4, :, :], w_sc_src[4 * q : 4 * q + 4].bitcast(I32))
 
         nc.scalar.copy(u_bf[:], u_raw[:].rearrange("p h j n -> p h n j"))
 
         nc.vector.tensor_copy(g_sc2[:], sc2[:].bitcast(U8).indirect(list2[:]))
         for q in range(4):
-            nc.scalar.dma_start(shifted2[QUAD * q : QUAD * q + 4, :], g_sc2[4 + 4 * q : 8 + 4 * q, :].bitcast(I32))
+            nc.scalar.dma_start(shifted2[QUAD * q : QUAD * q + 4, :], g_sc2[16 + 4 * q : 20 + 4 * q, :].bitcast(I32))
         nc.vector.tensor_copy(g_words2[:], words2[:].bitcast(U32).indirect(list2[:]))
-        sc1_u8 = sc1[:].rearrange("p a t -> p (a t)").bitcast(U8)
-        for a in range(KP):
-            nc.vector.tensor_copy(g_sc1[a][:], sc1_u8[:, T * a : T * (a + 1)].indirect(list1[:]))
         nc.vector.tensor_copy(
             parted2[:].bitcast(U16).rearrange("p (h n) -> p h n", h=LP),
             g_words2[:].bitcast(U16).rearrange("p (n h) -> p h n", h=LP),
         )
+        sc1_u8 = sc1[:].rearrange("p a t -> p (a t)").bitcast(U8)
+        for a in range(KP):
+            nc.vector.tensor_copy(g_sc1[a][:], sc1_u8[:, T * a : T * (a + 1)].indirect(list1[:]))
         u_codes = keep.tile([P, LP * M], U32, name="u_codes", tag="turns", align_bytes=64)
         nc.vector.quantize_mx(
             out=u_codes[:].bitcast(FP8X4),

@@ -30,14 +30,14 @@ def tile_list_tab48_none_kernel(tc, tab, w4_words, w4_scales, tab2, u, offs, off
         list1 = keep.tile([P, S // 16], U16, name="list1")
         list2 = keep.tile([P, S // 16], U16, name="list2")
         sc2 = keep.tile([P, T // 4], I32, name="sc2", align_bytes=64)
-        sc1 = keep.tile([P, KP, T // 4], I32, name="sc1", tag="turns", align_bytes=64)
+        sc1 = keep.tile([P, KP * T // 4 + 16], I32, name="sc1", tag="turns", align_bytes=64)
+        zero = keep.tile([P, 1], I32, name="zero", tag="zeros", align_bytes=64)
         words2 = keep.tile([P, T], I32, name="words2", align_bytes=64)
         words1 = [keep.tile([P, T], I32, name=f"words1_{a}", align_bytes=64) for a in range(KP)]
         u_raw = keep.tile([P, LP, 4, M], F32, name="u_raw", align_bytes=64)
         u_bf = keep.tile([P, LP, M, 4], BF16, name="u_bf", align_bytes=64)
         u_scales = keep.tile([P, LP * M], U8, name="u_scales", align_bytes=64)
         w_words = keep.tile([P, KP, 2 * M], U8, name="w_words", align_bytes=64)
-        w_sc = keep.tile([P, KP, M // 4], I32, name="w_sc", align_bytes=64)
         g_words2 = keep.tile([P, S], U32, name="g_words2", align_bytes=64)
         parted2 = keep.tile([P, LP * 2 * S], U8, name="parted2", align_bytes=64)
         g_sc2 = keep.tile([P, S], U8, name="g_sc2", align_bytes=64)
@@ -50,8 +50,11 @@ def tile_list_tab48_none_kernel(tc, tab, w4_words, w4_scales, tab2, u, offs, off
 
         nc.gpsimd.memset(shifted2[:], 0)
         nc.vector.memset(sc1[:], 0)
+        nc.gpsimd.memset(words2[:, 0:1], 0)
+        nc.vector.tensor_copy(zero[:], sc1[:, KP * T // 4 : KP * T // 4 + 1])
         for a in range(KP):
-            nc.vector.memset(words1[a][:, 0:1], 0)
+            nc.vector.tensor_copy(words1[a][:, 0:1], zero[:])
+        w_sc = keep.tile([P, KP, M // 4], I32, name="w_sc", tag="zeros", align_bytes=64)
         nc.vector.memset(w_sc[:], 0)
 
         def load_words(eng, tile, src):
@@ -68,8 +71,9 @@ def tile_list_tab48_none_kernel(tc, tab, w4_words, w4_scales, tab2, u, offs, off
         nc.gpsimd.dma_start(u_raw[:].rearrange("p h j n -> p h (j n)"), u.rearrange("(h p j) n -> p h (j n)", h=LP, j=4))
         nc.gpsimd.dma_start(w_words[:].bitcast(I32), w4_words.rearrange("a p b -> p a b").bitcast(I32))
         tab_sc = tab[:, 512 * T :].rearrange("a (q t) -> q a t", q=16)
+        sc1_planes = sc1[:, 0 : KP * T // 4].rearrange("p (a t) -> p a t", a=KP)
         for q in range(4):
-            nc.sync.dma_start(sc1[QUAD * q : QUAD * q + 4, :, :], tab_sc[4 * q : 4 * q + 4].bitcast(I32))
+            nc.sync.dma_start(sc1_planes[QUAD * q : QUAD * q + 4, :, :], tab_sc[4 * q : 4 * q + 4].bitcast(I32))
         for a in range(KP):
             load_words(nc.sync, words1[a], tab[a])
         w_sc_src = w4_scales.rearrange("a q n -> q a n")
@@ -86,7 +90,7 @@ def tile_list_tab48_none_kernel(tc, tab, w4_words, w4_scales, tab2, u, offs, off
             parted2[:].bitcast(U16).rearrange("p (h n) -> p h n", h=LP),
             g_words2[:].bitcast(U16).rearrange("p (n h) -> p h n", h=LP),
         )
-        sc1_u8 = sc1[:].rearrange("p a t -> p (a t)").bitcast(U8)
+        sc1_u8 = sc1[:].bitcast(U8)
         for a in range(KP):
             nc.vector.tensor_copy(g_sc1[a][:], sc1_u8[:, T * a : T * (a + 1)].indirect(list1[:]))
         u_codes = keep.tile([P, LP * M], U32, name="u_codes", tag="turns", align_bytes=64)

@@ -100,7 +100,9 @@ def tile_list_tab48_none_kernel(tc, tab, w4_words, w4_scales, tab2, u, offs, off
             in_=u_bf[:].rearrange("p h n j -> p (h n j)"),
         )
         shifted2_u8 = shifted2[:].bitcast(U8)
-        for h in range(LP):
+        w_sc_u8 = w_sc[:].rearrange("p a n -> p (a n)").bitcast(U8)
+
+        def multiply2(h):
             plane = (g_sc2[:], shifted2_u8)[h]
             for g in range(GROUPS):
                 nc.tensor.matmul_mx(
@@ -113,32 +115,33 @@ def tile_list_tab48_none_kernel(tc, tab, w4_words, w4_scales, tab2, u, offs, off
                     stop=False,
                 )
 
-        w_sc_u8 = w_sc[:].rearrange("p a n -> p (a n)").bitcast(U8)
+        def gather_and_multiply(a, pieces):
+            done = 0
+            for piece in pieces:
+                nc.vector.tensor_copy(
+                    g_words1[a][:, done : done + piece],
+                    words1[a][:].bitcast(U32).indirect(list1[:, done // 16 : (done + piece) // 16]),
+                )
+                for g in range(done // GROUP, (done + piece) // GROUP):
+                    nc.tensor.matmul_mx(
+                        out=banks[g][:, 0:GROUP],
+                        lhsT=w_words[:, a, :].bitcast(FP4X4),
+                        lhsT_scale=w_sc_u8[:, M * a : M * (a + 1)],
+                        rhs=g_words1[a][:, GROUP * g : GROUP * (g + 1)].bitcast(FP8X4),
+                        rhs_scale=g_sc1[a][:, GROUP * g : GROUP * (g + 1)],
+                        start=False,
+                        stop=(a == KP - 1),
+                    )
+                done += piece
 
-        def multiply(a, g):
-            nc.tensor.matmul_mx(
-                out=banks[g][:, 0:GROUP],
-                lhsT=w_words[:, a, :].bitcast(FP4X4),
-                lhsT_scale=w_sc_u8[:, M * a : M * (a + 1)],
-                rhs=g_words1[a][:, GROUP * g : GROUP * (g + 1)].bitcast(FP8X4),
-                rhs_scale=g_sc1[a][:, GROUP * g : GROUP * (g + 1)],
-                start=False,
-                stop=(a == KP - 1),
-            )
-
-        for a in range(KP - 1):
-            nc.vector.tensor_copy(g_words1[a][:], words1[a][:].bitcast(U32).indirect(list1[:]))
-            for g in range(GROUPS):
-                multiply(a, g)
-        a = KP - 1
+        multiply2(0)
+        gather_and_multiply(0, (S,))
+        multiply2(1)
+        gather_and_multiply(1, (S,))
+        gather_and_multiply(2, (2 * GROUP, GROUP, GROUP))
         cut = S - GROUP
-        nc.vector.tensor_copy(g_words1[a][:, 0:cut], words1[a][:].bitcast(U32).indirect(list1[:, 0 : cut // 16]))
-        for g in range(GROUPS - 1):
-            multiply(a, g)
-        nc.vector.tensor_copy(g_words1[a][:, cut:S], words1[a][:].bitcast(U32).indirect(list1[:, cut // 16 :]))
-        multiply(a, GROUPS - 1)
         for g in range(GROUPS - 1):
             nc.scalar.copy(out_a[:, GROUP * g : GROUP * (g + 1)], banks[g][:, 0:GROUP])
         nc.sync.dma_start(out[:, 0:cut], out_a[:])
         nc.vector.tensor_copy(out_b[:], banks[GROUPS - 1][:, 0:GROUP])
-        nc.sync.dma_start(out[:, cut:S], out_b[:])
+        nc.scalar.dma_start(out[:, cut:S], out_b[:])

from contextlib import ExitStack

import concourse.mybir as mybir

F32 = mybir.dt.float32
BF16 = mybir.dt.bfloat16
I32 = mybir.dt.int32
U32 = mybir.dt.uint32
U16 = mybir.dt.uint16
U8 = mybir.dt.uint8
FP8X4 = mybir.dt.float8_e4m3fn_x4
FP4X4 = mybir.dt.float4_e2m1fn_x4

P = 128
K, L, M, T, S = 1536, 1024, 128, 1024, 512
KP = K // 512
LP = L // 512
QUAD = 32
GROUP = 128
GROUPS = S // GROUP
FLOPS = 2 * M * S * (K + L)


def tile_list_tab48_none_kernel(tc, tab, w4_words, w4_scales, tab2, u, offs, offs2, out):
    nc = tc.nc
    with ExitStack() as ctx:
        keep = ctx.enter_context(tc.tile_pool(name="keep", bufs=1))
        psum = ctx.enter_context(tc.psum_pool(name="psum", bufs=1))

        list1 = keep.tile([P, S // 16], U16, name="list1")
        list2 = keep.tile([P, S // 16], U16, name="list2")
        sc2 = keep.tile([P, T // 4], I32, name="sc2", align_bytes=64)
        sc1 = keep.tile([P, KP * T // 4 + 16], I32, name="sc1", tag="turns", align_bytes=64)
        zero = keep.tile([P, 1], I32, name="zero", tag="zeros", align_bytes=64)
        words2 = keep.tile([P, T], I32, name="words2", align_bytes=64)
        words1 = [keep.tile([P, T], I32, name=f"words1_{a}", align_bytes=64) for a in range(KP)]
        u_raw = keep.tile([P, LP, 4, M], F32, name="u_raw", align_bytes=64)
        u_bf = keep.tile([P, LP, M, 4], BF16, name="u_bf", align_bytes=64)
        u_scales = keep.tile([P, LP * M], U8, name="u_scales", align_bytes=64)
        w_words = keep.tile([P, KP, 2 * M], U8, name="w_words", align_bytes=64)
        g_words2 = keep.tile([P, S], U32, name="g_words2", align_bytes=64)
        parted2 = keep.tile([P, LP * 2 * S], U8, name="parted2", align_bytes=64)
        g_sc2 = keep.tile([P, S], U8, name="g_sc2", align_bytes=64)
        shifted2 = keep.tile([P, S // 4], I32, name="shifted2", align_bytes=64)
        g_words1 = [keep.tile([P, S], U32, name=f"g_words1_{a}", align_bytes=64) for a in range(KP)]
        g_sc1 = [keep.tile([P, S], U8, name=f"g_sc1_{a}", align_bytes=64) for a in range(KP)]
        out_a = keep.tile([P, S - GROUP], F32, name="out_a", align_bytes=64)
        out_b = keep.tile([P, GROUP], F32, name="out_b", align_bytes=64)
        banks = [psum.tile([P, 512], F32, name=f"bank{g}") for g in range(GROUPS)]

        nc.gpsimd.memset(shifted2[:], 0)
        nc.vector.memset(sc1[:], 0)
        nc.gpsimd.memset(words2[:, 0:1], 0)
        nc.vector.tensor_copy(zero[:], sc1[:, KP * T // 4 : KP * T // 4 + 1])
        for a in range(KP):
            nc.vector.tensor_copy(words1[a][:, 0:1], zero[:])
        w_sc = keep.tile([P, KP, M // 4], I32, name="w_sc", tag="zeros", align_bytes=64)
        nc.vector.memset(w_sc[:], 0)

        def load_words(eng, tile, src):
            eng.dma_start(tile[:], src[0 : 512 * T].rearrange("(p b) -> p b", p=P).bitcast(I32))

        nc.sync.dma_start(list2[:], offs2)
        tab2_sc = tab2[0, 512 * T :].rearrange("(r t) -> r t", t=T).bitcast(I32)
        nc.sync.dma_start(sc2[0:QUAD, :], tab2_sc)
        for q in range(1, 4):
            rows = tab2_sc[4 * q : 4 * q + 4, :].unsqueeze(0).to_broadcast([8, 4, T // 4])
            nc.sync.dma_start(sc2[QUAD * q : QUAD * (q + 1), :], rows)
        load_words(nc.sync, words2, tab2[0])
        nc.sync.dma_start(list1[:], offs)
        nc.gpsimd.dma_start(u_raw[:].rearrange("p h j n -> p h (j n)"), u.rearrange("(h p j) n -> p h (j n)", h=LP, j=4))
        nc.gpsimd.dma_start(w_words[:].bitcast(I32), w4_words.rearrange("a p b -> p a b").bitcast(I32))
        tab_sc = tab[:, 512 * T :].rearrange("a (q t) -> q a t", q=16)
        sc1_planes = sc1[:, 0 : KP * T // 4].rearrange("p (a t) -> p a t", a=KP)
        for q in range(4):
            nc.sync.dma_start(sc1_planes[QUAD * q : QUAD * q + 4, :, :], tab_sc[4 * q : 4 * q + 4].bitcast(I32))
        for a in range(KP):
            load_words(nc.sync, words1[a], tab[a])
        w_sc_src = w4_scales.rearrange("a q n -> q a n")
        for q in range(4):
            nc.sync.dma_start(w_sc[QUAD * q : QUAD * q + 4, :, :], w_sc_src[4 * q : 4 * q + 4].bitcast(I32))

        nc.scalar.copy(u_bf[:], u_raw[:].rearrange("p h j n -> p h n j"))

        nc.vector.tensor_copy(g_sc2[:], sc2[:].bitcast(U8).indirect(list2[:]))
        for q in range(4):
            nc.scalar.dma_start(shifted2[QUAD * q : QUAD * q + 4, :], g_sc2[16 + 4 * q : 20 + 4 * q, :].bitcast(I32))
        nc.vector.tensor_copy(g_words2[:], words2[:].bitcast(U32).indirect(list2[:]))
        nc.vector.tensor_copy(
            parted2[:].bitcast(U16).rearrange("p (h n) -> p h n", h=LP),
            g_words2[:].bitcast(U16).rearrange("p (n h) -> p h n", h=LP),
        )
        sc1_u8 = sc1[:].bitcast(U8)
        for a in range(KP):
            nc.vector.tensor_copy(g_sc1[a][:], sc1_u8[:, T * a : T * (a + 1)].indirect(list1[:]))
        u_codes = keep.tile([P, LP * M], U32, name="u_codes", tag="turns", align_bytes=64)
        nc.vector.quantize_mx(
            out=u_codes[:].bitcast(FP8X4),
            scales=u_scales[:],
            in_=u_bf[:].rearrange("p h n j -> p (h n j)"),
        )
        shifted2_u8 = shifted2[:].bitcast(U8)
        w_sc_u8 = w_sc[:].rearrange("p a n -> p (a n)").bitcast(U8)

        def multiply2(h):
            plane = (g_sc2[:], shifted2_u8)[h]
            for g in range(GROUPS):
                nc.tensor.matmul_mx(
                    out=banks[g][:, 0:GROUP],
                    lhsT=u_codes[:, M * h : M * (h + 1)].bitcast(FP8X4),
                    lhsT_scale=u_scales[:, M * h : M * (h + 1)],
                    rhs=parted2[:, 2 * S * h + 2 * GROUP * g : 2 * S * h + 2 * GROUP * (g + 1)].bitcast(FP4X4),
                    rhs_scale=plane[:, GROUP * g : GROUP * (g + 1)],
                    start=(h == 0),
                    stop=False,
                )

        def gather_and_multiply(a, pieces):
            done = 0
            for piece in pieces:
                nc.vector.tensor_copy(
                    g_words1[a][:, done : done + piece],
                    words1[a][:].bitcast(U32).indirect(list1[:, done // 16 : (done + piece) // 16]),
                )
                for g in range(done // GROUP, (done + piece) // GROUP):
                    nc.tensor.matmul_mx(
                        out=banks[g][:, 0:GROUP],
                        lhsT=w_words[:, a, :].bitcast(FP4X4),
                        lhsT_scale=w_sc_u8[:, M * a : M * (a + 1)],
                        rhs=g_words1[a][:, GROUP * g : GROUP * (g + 1)].bitcast(FP8X4),
                        rhs_scale=g_sc1[a][:, GROUP * g : GROUP * (g + 1)],
                        start=False,
                        stop=(a == KP - 1),
                    )
                done += piece

        multiply2(0)
        gather_and_multiply(0, (S,))
        multiply2(1)
        gather_and_multiply(1, (S,))
        gather_and_multiply(2, (2 * GROUP, GROUP, GROUP))
        cut = S - GROUP
        for g in range(GROUPS - 1):
            nc.scalar.copy(out_a[:, GROUP * g : GROUP * (g + 1)], banks[g][:, 0:GROUP])
        nc.sync.dma_start(out[:, 0:cut], out_a[:])
        nc.vector.tensor_copy(out_b[:], banks[GROUPS - 1][:, 0:GROUP])
        nc.scalar.dma_start(out[:, cut:S], out_b[:])
